import numpy as np
import ml_dtypes


def mxq(x, axis, fmt="e4m3"):
    dtype, down = {"e4m3": (ml_dtypes.float8_e4m3fn, 7), "e5m2": (ml_dtypes.float8_e5m2, 14)}[fmt]
    v = np.moveaxis(np.asarray(x, np.float32).astype(ml_dtypes.bfloat16).astype(np.float64), axis, -1)
    blocks = v.reshape(v.shape[:-1] + (-1, 32))
    amax = np.abs(blocks).max(-1, keepdims=True)
    byte = np.maximum(np.where(amax > 0, np.frexp(amax)[1] - 1 + 127, 0) - down, 1)
    scale = np.exp2(byte - 127.0)
    codes = (blocks / scale).astype(np.float32).astype(dtype).astype(np.float64)
    return np.moveaxis((codes * scale).reshape(v.shape), -1, axis)


WIDE = False


def mx_kscale(k):
    if not WIDE:
        return np.ones(k)
    levels = np.array([10, -10, 5, -5, 0])
    if k % 512:
        return np.exp2(np.random.permutation(np.resize(levels, k // 32))).repeat(32)
    a = np.empty((k // 512, 16))
    for p in range(k // 512):
        a[p, :8] = np.random.permutation(np.resize(levels, 8))
        for g in range(8):
            far = levels[np.abs(levels - a[p, g]) >= 10]
            a[p, g + 8] = far[np.random.randint(len(far))]
    return np.exp2(a.ravel()).repeat(32)


def f64(x):
    return np.asarray(x).astype(np.float64)


def striped(idx):
    return np.tile(idx.reshape(-1, 16).T, (8, 1)).astype(np.uint16)


def unstriped(offs):
    return offs[:16].T.reshape(-1).astype(np.int64)


def pack_weight(w):
    k, n = w.shape
    w = f64(np.asarray(w, np.float32).astype(ml_dtypes.bfloat16)).reshape(k // 32, 32, n)
    amax = np.abs(w).max(1)
    byte = np.clip(np.where(amax > 0, np.frexp(amax)[1] - 1 + 127 - 7, 1), 1, 254)
    scaled = (w * np.exp2(127.0 - byte)[:, None, :]).reshape(k, n).astype(np.float32)
    words = np.ascontiguousarray(scaled.reshape(k // 512, 128, 4, n).transpose(0, 1, 3, 2)).astype(ml_dtypes.float8_e4m3fn).view(np.uint8)
    return words, np.ascontiguousarray(byte.astype(np.uint8).reshape(k // 512, 16, n))


def unpack_weight(words, scales):
    g, p, n, _ = words.shape
    vals = np.ascontiguousarray(words).view(ml_dtypes.float8_e4m3fn).astype(np.float64) * np.repeat(np.exp2(scales.astype(np.float64) - 127.0), 8, axis=1)[..., None]
    return vals.transpose(0, 1, 3, 2).reshape(g * 512, n)


K, T, S, N, U, D = 512, 2048, 512, 256, 1024, 4
P = 2 ** 7


def setup_inputs():
    n = np.random.standard_normal
    s = mx_kscale(K)[:, None]
    packed_xT = pack_weight(n((K, T)) * s)
    return {
        "x_words": packed_xT[0],
        "x_scales": packed_xT[1],
        "w1": (n((K, N)) / np.sqrt(K) / s).astype(np.float32),
        "free": (np.tile(np.random.uniform(0.3, 1.2, S), (P, 1))).astype(np.float32),
        "theta": (-np.random.uniform(0.8, 2.0, (N, 1))).astype(np.float32),
        "offs": striped(np.random.permutation(T)[:S]),
        "lka": striped(np.random.permutation(np.concatenate([np.arange(S), np.random.randint(0, S, U - S)]))),
        "lkb": striped(np.random.permutation(np.concatenate([np.arange(S), np.random.randint(0, S, U - S)]))),
    }


def reference(x_words, x_scales, w1, free, theta, offs, lka, lkb):
    xq = unpack_weight(x_words, x_scales)[:, unstriped(offs)]
    y = mxq(f64(w1), 0, "e4m3").T @ xq
    load = 0.9 * (np.log(np.exp(y) + 1.0))
    time = f64(free)[:1] * (0.15 * (((load) ** 2) ** 2) + 1.0)
    rt = time[:, unstriped(lka)] + time[:, unstriped(lkb)]
    ut = f64(theta) * rt
    top = ut.reshape(len(ut), -1, D).max(axis=2)
    ex = np.exp(ut - np.repeat(top, D, axis=1))
    total = ex.reshape(len(ex), -1, D).sum(axis=2)
    share = ex / np.repeat(total, D, axis=1)
    pr = share * rt
    return pr.reshape(len(pr), -1, D).sum(axis=2)

@@ -1,0 +1,223 @@
+from contextlib import ExitStack
+
+import concourse.mybir as mybir
+from concourse.masks import make_identity
+
+F32 = mybir.dt.float32
+BF16 = mybir.dt.bfloat16
+I32 = mybir.dt.int32
+U32 = mybir.dt.uint32
+U16 = mybir.dt.uint16
+U8 = mybir.dt.uint8
+FP8X4 = mybir.dt.float8_e4m3fn_x4
+ALU = mybir.AluOpType
+ACT = mybir.ActivationFunctionType
+AX = mybir.AxisListType
+
+P = 128
+K, T, S, N, U, D = 512, 2048, 512, 256, 1024, 4
+HALF = S // 2
+TRIPS = U // D
+PIECE = P * D
+SPARE = 8
+EXP_CAP = 2.0 ** 60
+LOAD_FACTOR = 0.9 * 0.15 ** 0.25
+THETA_FOR_ZERO = 2.0 ** -40
+
+FLOPS = 2 * K * S * N
+
+
+def tile_picked_ybpr_time_p_kernel(
+    tc, x_words, x_scales, w1, free, theta, offs, lka, lkb, out
+):
+    nc = tc.nc
+    with ExitStack() as ctx:
+        keep = ctx.enter_context(tc.tile_pool(name="keep", bufs=1))
+        ring = ctx.enter_context(tc.tile_pool(name="ring", bufs=2))
+        psum = ctx.enter_context(tc.psum_pool(name="psum", bufs=1))
+
+        offs_t = keep.tile([P, S // 16], U16)
+        lka_t = keep.tile([P, U // 16], U16)
+        lkb_t = keep.tile([P, U // 16], U16)
+        words = keep.tile([P, T], I32, align_bytes=64)
+        scales = keep.tile([P, T], U8, align_bytes=64)
+        w_raw = keep.tile([P, 4, N], F32)
+        theta_t = keep.tile([P, 2], F32)
+        free_t = keep.tile([P, S], F32)
+
+        nc.vector.memset(scales[:].bitcast(I32), 0)
+        nc.sync.dma_start(out=w_raw[:], in_=w1.rearrange("(p j) n -> p j n", j=4))
+        nc.sync.dma_start(offs_t[:], offs)
+        for q in range(4):
+            nc.sync.dma_start(
+                out=scales[32 * q : 32 * q + 4, :].bitcast(I32),
+                in_=x_scales[0, 4 * q : 4 * q + 4, :].bitcast(I32),
+            )
+        nc.sync.dma_start(out=words[:], in_=x_words[0].rearrange("p n t -> p (n t)").bitcast(I32))
+        with nc.allow_non_contiguous_dma(reason="one value a partition"):
+            nc.sync.dma_start(out=theta_t[:], in_=theta.rearrange("(b p) o -> p (b o)", p=P))
+        nc.sync.dma_start(out=free_t[:], in_=free)
+        nc.sync.dma_start(lka_t[:], lka)
+        nc.sync.dma_start(lkb_t[:], lkb)
+
+        ident = keep.tile([P, P], F32)
+        make_identity(nc, ident[:])
+
+        u = [keep.tile([P, S + SPARE], F32, name=f"u{b}") for b in range(2)]
+        for b in range(2):
+            nc.vector.memset(u[b][:, S:], 0.0)
+
+        w_bf = keep.tile([P, N, 4], BF16, align_bytes=64)
+        nc.vector.tensor_copy(out=w_bf[:], in_=w_raw[:].rearrange("p j n -> p n j"))
+        x_sc = keep.tile([P, S], U8, align_bytes=64)
+        nc.vector.tensor_copy(x_sc[:], scales[:].indirect(offs_t[:]))
+        w_q = keep.tile([P, N], U32, align_bytes=64)
+        w_sc = keep.tile([P, N], U8, align_bytes=64)
+        nc.vector.quantize_mx(
+            out=w_q[:].bitcast(FP8X4), scales=w_sc[:], in_=w_bf[:].rearrange("p n j -> p (n j)")
+        )
+
+        x_q = [keep.tile([P, HALF], U32, name=f"x_q{h}", align_bytes=64) for h in range(2)]
+        y = [psum.tile([P, 2, HALF], F32, name=f"y{h}") for h in range(2)]
+        e = keep.tile([P, 2, S], F32)
+        for h in range(2):
+            nc.vector.tensor_copy(
+                x_q[h][:], words[:].bitcast(U32).indirect(offs_t[:, 16 * h : 16 * (h + 1)])
+            )
+            for b in range(2):
+                nc.tensor.matmul_mx(
+                    out=y[h][:, b, :],
+                    lhsT=w_q[:, P * b : P * (b + 1)].bitcast(FP8X4),
+                    lhsT_scale=w_sc[:, P * b : P * (b + 1)],
+                    rhs=x_q[h][:].bitcast(FP8X4),
+                    rhs_scale=x_sc[:, HALF * h : HALF * (h + 1)],
+                    start=True,
+                    stop=True,
+                )
+            nc.scalar.activation(e[:, :, HALF * h : HALF * (h + 1)], y[h][:], ACT.Exp)
+
+        is_zero = keep.tile([P, 2], F32)
+        nc.vector.tensor_scalar(is_zero[:], theta_t[:], 0.0, THETA_FOR_ZERO, ALU.is_equal, ALU.mult)
+        theta_nz = keep.tile([P, 2], F32)
+        nc.vector.tensor_tensor(theta_nz[:], theta_t[:], is_zero[:], ALU.add)
+        inv_theta = keep.tile([P, 2], F32)
+        nc.vector.reciprocal(inv_theta[:], theta_nz[:])
+        neg_inv_theta = keep.tile([P, 2], F32)
+        nc.vector.tensor_scalar(neg_inv_theta[:], inv_theta[:], -1.0, 0.0, ALU.mult, ALU.add)
+
+        e1 = keep.tile([P, 2, S], F32)
+        nc.vector.tensor_scalar(e1[:], e[:], EXP_CAP, 1.0, ALU.min, ALU.add)
+        g = keep.tile([P, 2, S], F32)
+        for b in range(2):
+            nc.vector.tensor_scalar(g[:, b, :], free_t[:], theta_nz[:, b : b + 1], 0.0, ALU.mult, ALU.add)
+
+        lg = keep.tile([P, 2, S], F32)
+        sp = keep.tile([P, 2, S], F32)
+        s2 = keep.tile([P, 2, S], F32)
+        s4 = keep.tile([P, 2, S], F32)
+        cols = [slice(HALF * h, HALF * (h + 1)) for h in range(2)]
+        for h in range(2):
+            nc.scalar.activation(lg[:, 0, cols[h]], e1[:, 0, cols[h]], ACT.Ln)
+        for h in range(2):
+            nc.vector.tensor_tensor(sp[:, 0, cols[h]], y[h][:, 0, :], lg[:, 0, cols[h]], ALU.max)
+        nc.scalar.activation(lg[:, 1, :], e1[:, 1, :], ACT.Ln)
+        for h in range(2):
+            nc.vector.scalar_tensor_tensor(
+                s2[:, 0, cols[h]], sp[:, 0, cols[h]], LOAD_FACTOR ** 2, sp[:, 0, cols[h]], ALU.mult, ALU.mult
+            )
+            nc.scalar.activation(s4[:, 0, cols[h]], s2[:, 0, cols[h]], ACT.Square)
+        for h in range(2):
+            nc.vector.tensor_tensor(sp[:, 1, cols[h]], y[h][:, 1, :], lg[:, 1, cols[h]], ALU.max)
+            nc.vector.scalar_tensor_tensor(
+                u[0][:, cols[h]], s4[:, 0, cols[h]], 1.0, g[:, 0, cols[h]], ALU.add, ALU.mult
+            )
+        nc.scalar.activation(s2[:, 1, :], sp[:, 1, :], ACT.Square, scale=LOAD_FACTOR)
+        nc.scalar.activation(s4[:, 1, :], s2[:, 1, :], ACT.Square)
+
+        neg_top = keep.tile([P, 2, TRIPS], F32)
+        sums = [psum.tile([P, 2, TRIPS], F32, name=f"sums{b}") for b in range(2)]
+        res = [keep.tile([P, TRIPS], F32, name=f"res{b}") for b in range(2)]
+        state = {}
+
+        def gather_first(i):
+            b, h = divmod(i, 2)
+            first = ring.tile([P, PIECE], F32, name="first")
+            nc.vector.tensor_copy(first[:], u[b][:].indirect(lka_t[:, 32 * h : 32 * (h + 1)]))
+            state[i, "first"] = first
+
+        def gather_second(i):
+            b, h = divmod(i, 2)
+            ut = ring.tile([P, PIECE], F32, name="ut")
+            nc.vector.tensor_tensor(
+                ut[:], u[b][:].indirect(lkb_t[:, 32 * h : 32 * (h + 1)]), state[i, "first"][:], ALU.add
+            )
+            state[i, "ut"] = ut
+
+        def shift(i):
+            b, h = divmod(i, 2)
+            ut = state[i, "ut"]
+            top = neg_top[:, b, P * h : P * (h + 1)]
+            nc.vector.tensor_reduce(
+                top, ut[:].rearrange("p (v d) -> p v d", d=D), AX.X, ALU.max, negate=True
+            )
+            delta = psum.tile([P, D, P], F32, name=f"delta{i % 2}")
+            for d in range(D):
+                nc.tensor.matmul(delta[:, d, :], ut[:, d::D], ident[:], start=True, stop=False, is_transpose=True)
+                nc.tensor.matmul(delta[:, d, :], top, ident[:], start=False, stop=True, is_transpose=True)
+            ex = ring.tile([P, D, P], F32, name="ex")
+            nc.scalar.activation(ex[:], delta[:], ACT.Exp)
+            for d in range(D):
+                nc.tensor.matmul(
+                    sums[b][:, 0, P * h : P * (h + 1)], ex[:, d, :], ident[:],
+                    start=(d == 0), stop=(d == D - 1), is_transpose=True,
+                )
+            state[i, "delta"] = delta
+            state[i, "ex"] = ex
+
+        def weigh(i):
+            b, h = divmod(i, 2)
+            pr = ring.tile([P, D, P], F32, name="pr")
+            nc.vector.tensor_tensor(pr[:], state[i, "delta"][:], state[i, "ex"][:], ALU.mult)
+            for d in range(D):
+                nc.tensor.matmul(
+                    sums[b][:, 1, P * h : P * (h + 1)], pr[:, d, :], ident[:],
+                    start=(d == 0), stop=(d == D - 1), is_transpose=True,
+                )
+
+        def finish(b, c, inv_total):
+            mean = ring.tile([P, TRIPS], F32, name="mean")
+            nc.vector.scalar_tensor_tensor(
+                mean[:, c], sums[b][:, 1, c], inv_theta[:, b : b + 1], inv_total, ALU.mult, ALU.mult
+            )
+            nc.vector.scalar_tensor_tensor(
+                res[b][:, c], neg_top[:, b, c], neg_inv_theta[:, b : b + 1], mean[:, c], ALU.mult, ALU.add
+            )
+            nc.sync.dma_start(out=out[P * b : P * (b + 1), c], in_=res[b][:, c])
+
+        gather_first(0)
+        nc.vector.scalar_tensor_tensor(u[1][:, :S], s4[:, 1, :], 1.0, g[:, 1, :], ALU.add, ALU.mult)
+        gather_second(0)
+        gather_first(1)
+        shift(0)
+        gather_second(1)
+        gather_first(2)
+        shift(1)
+        weigh(0)
+        gather_second(2)
+        gather_first(3)
+        weigh(1)
+        root = keep.tile([P, TRIPS], F32)
+        nc.scalar.activation(root[:], sums[0][:, 0, :], ACT.Abs_reciprocal_sqrt)
+        inv0 = keep.tile([P, TRIPS], F32)
+        nc.scalar.activation(inv0[:], root[:], ACT.Square)
+        shift(2)
+        gather_second(3)
+        finish(0, slice(0, TRIPS), inv0[:])
+        shift(3)
+        weigh(2)
+        inv1 = keep.tile([P, TRIPS], F32)
+        nc.vector.reciprocal(inv1[:, :P], sums[1][:, 0, :P])
+        finish(1, slice(0, P), inv1[:, :P])
+        weigh(3)
+        nc.vector.reciprocal(inv1[:, P:], sums[1][:, 0, P:])
+        finish(1, slice(P, TRIPS), inv1[:, P:])

@@ -1,3 +1,4 @@
+import math
 from contextlib import ExitStack
 
 import concourse.mybir as mybir
@@ -22,6 +23,8 @@ PIECE = P * D
 SPARE = 8
 EXP_CAP = 2.0 ** 60
 LOAD_FACTOR = 0.9 * 0.15 ** 0.25
+LOG_CAP = math.log(1.0 + EXP_CAP)
+CAP_TIME = 1.0 + (LOAD_FACTOR * LOG_CAP) ** 4
 THETA_FOR_ZERO = 2.0 ** -40
 
 FLOPS = 2 * K * S * N
@@ -45,17 +48,17 @@ def tile_picked_ybpr_time_p_kernel(
         theta_t = keep.tile([P, 2], F32)
         free_t = keep.tile([P, S], F32)
 
-        nc.vector.memset(scales[:].bitcast(I32), 0)
-        nc.sync.dma_start(out=w_raw[:], in_=w1.rearrange("(p j) n -> p j n", j=4))
+        nc.gpsimd.memset(scales[:].bitcast(I32), 0)
         nc.sync.dma_start(offs_t[:], offs)
+        nc.sync.dma_start(out=w_raw[:], in_=w1.rearrange("(p j) n -> p j n", j=4))
+        with nc.allow_non_contiguous_dma(reason="one value a partition"):
+            nc.sync.dma_start(out=theta_t[:], in_=theta.rearrange("(b p) o -> p (b o)", p=P))
         for q in range(4):
             nc.sync.dma_start(
                 out=scales[32 * q : 32 * q + 4, :].bitcast(I32),
                 in_=x_scales[0, 4 * q : 4 * q + 4, :].bitcast(I32),
             )
         nc.sync.dma_start(out=words[:], in_=x_words[0].rearrange("p n t -> p (n t)").bitcast(I32))
-        with nc.allow_non_contiguous_dma(reason="one value a partition"):
-            nc.sync.dma_start(out=theta_t[:], in_=theta.rearrange("(b p) o -> p (b o)", p=P))
         nc.sync.dma_start(out=free_t[:], in_=free)
         nc.sync.dma_start(lka_t[:], lka)
         nc.sync.dma_start(lkb_t[:], lkb)
@@ -77,66 +80,69 @@ def tile_picked_ybpr_time_p_kernel(
             out=w_q[:].bitcast(FP8X4), scales=w_sc[:], in_=w_bf[:].rearrange("p n j -> p (n j)")
         )
 
-        x_q = [keep.tile([P, HALF], U32, name=f"x_q{h}", align_bytes=64) for h in range(2)]
-        y = [psum.tile([P, 2, HALF], F32, name=f"y{h}") for h in range(2)]
-        e = keep.tile([P, 2, S], F32)
-        for h in range(2):
-            nc.vector.tensor_copy(
-                x_q[h][:], words[:].bitcast(U32).indirect(offs_t[:, 16 * h : 16 * (h + 1)])
-            )
-            for b in range(2):
-                nc.tensor.matmul_mx(
-                    out=y[h][:, b, :],
-                    lhsT=w_q[:, P * b : P * (b + 1)].bitcast(FP8X4),
-                    lhsT_scale=w_sc[:, P * b : P * (b + 1)],
-                    rhs=x_q[h][:].bitcast(FP8X4),
-                    rhs_scale=x_sc[:, HALF * h : HALF * (h + 1)],
-                    start=True,
-                    stop=True,
-                )
-            nc.scalar.activation(e[:, :, HALF * h : HALF * (h + 1)], y[h][:], ACT.Exp)
-
         is_zero = keep.tile([P, 2], F32)
         nc.vector.tensor_scalar(is_zero[:], theta_t[:], 0.0, THETA_FOR_ZERO, ALU.is_equal, ALU.mult)
         theta_nz = keep.tile([P, 2], F32)
         nc.vector.tensor_tensor(theta_nz[:], theta_t[:], is_zero[:], ALU.add)
         inv_theta = keep.tile([P, 2], F32)
         nc.vector.reciprocal(inv_theta[:], theta_nz[:])
-        neg_inv_theta = keep.tile([P, 2], F32)
-        nc.vector.tensor_scalar(neg_inv_theta[:], inv_theta[:], -1.0, 0.0, ALU.mult, ALU.add)
 
+        theta_cap = keep.tile([P, 1], F32)
+        nc.vector.tensor_scalar(theta_cap[:], theta_nz[:, 0:1], 1.0 / CAP_TIME, 1.0, ALU.mult, ALU.mult)
+
+        cols = [slice(HALF * h, HALF * (h + 1)) for h in range(2)]
+        x_q = [keep.tile([P, HALF], U32, name=f"x_q{h}", align_bytes=64) for h in range(2)]
+        y = {}
+        e = keep.tile([P, 2, S], F32)
+        for h in range(2):
+            nc.vector.tensor_copy(
+                x_q[h][:], words[:].bitcast(U32).indirect(offs_t[:, 16 * h : 16 * (h + 1)])
+            )
+            for b in range(2):
+                y[b, h] = psum.tile([P, HALF], F32, name=f"bank{2 * b + h}")
+                nc.tensor.matmul_mx(
+                    out=y[b, h][:],
+                    lhsT=w_q[:, P * b : P * (b + 1)].bitcast(FP8X4),
+                    lhsT_scale=w_sc[:, P * b : P * (b + 1)],
+                    rhs=x_q[h][:].bitcast(FP8X4),
+                    rhs_scale=x_sc[:, cols[h]],
+                    start=True,
+                    stop=True,
+                )
+                nc.scalar.activation(e[:, b, cols[h]], y[b, h][:], ACT.Exp)
+
+        big = keep.tile([P, S], F32)
+        for h in range(2):
+            nc.vector.tensor_scalar(big[:, cols[h]], y[0, h][:], LOG_CAP, LOAD_FACTOR, ALU.max, ALU.mult)
+        big2 = keep.tile([P, S], F32)
+        nc.vector.tensor_tensor(big2[:], big[:], big[:], ALU.mult)
         e1 = keep.tile([P, 2, S], F32)
         nc.vector.tensor_scalar(e1[:], e[:], EXP_CAP, 1.0, ALU.min, ALU.add)
-        g = keep.tile([P, 2, S], F32)
-        for b in range(2):
-            nc.vector.tensor_scalar(g[:, b, :], free_t[:], theta_nz[:, b : b + 1], 0.0, ALU.mult, ALU.add)
+        big4 = keep.tile([P, S], F32)
+        nc.vector.tensor_tensor(big4[:], big2[:], big2[:], ALU.mult)
+        over = keep.tile([P, S], F32)
+        nc.vector.tensor_scalar(over[:], big4[:], theta_cap[:], theta_cap[:], ALU.mult, ALU.add)
+        g0 = keep.tile([P, S], F32)
+        nc.vector.tensor_tensor(g0[:], over[:], free_t[:], ALU.mult)
 
         lg = keep.tile([P, 2, S], F32)
-        sp = keep.tile([P, 2, S], F32)
+        sp = keep.tile([P, S], F32)
         s2 = keep.tile([P, 2, S], F32)
         s4 = keep.tile([P, 2, S], F32)
-        cols = [slice(HALF * h, HALF * (h + 1)) for h in range(2)]
         for h in range(2):
             nc.scalar.activation(lg[:, 0, cols[h]], e1[:, 0, cols[h]], ACT.Ln)
         for h in range(2):
-            nc.vector.tensor_tensor(sp[:, 0, cols[h]], y[h][:, 0, :], lg[:, 0, cols[h]], ALU.max)
-        nc.scalar.activation(lg[:, 1, :], e1[:, 1, :], ACT.Ln)
+            nc.scalar.activation(s2[:, 0, cols[h]], lg[:, 0, cols[h]], ACT.Square, scale=LOAD_FACTOR)
         for h in range(2):
-            nc.vector.scalar_tensor_tensor(
-                s2[:, 0, cols[h]], sp[:, 0, cols[h]], LOAD_FACTOR ** 2, sp[:, 0, cols[h]], ALU.mult, ALU.mult
-            )
             nc.scalar.activation(s4[:, 0, cols[h]], s2[:, 0, cols[h]], ACT.Square)
-        for h in range(2):
-            nc.vector.tensor_tensor(sp[:, 1, cols[h]], y[h][:, 1, :], lg[:, 1, cols[h]], ALU.max)
             nc.vector.scalar_tensor_tensor(
-                u[0][:, cols[h]], s4[:, 0, cols[h]], 1.0, g[:, 0, cols[h]], ALU.add, ALU.mult
+                u[0][:, cols[h]], s4[:, 0, cols[h]], 1.0, g0[:, cols[h]], ALU.add, ALU.mult
             )
-        nc.scalar.activation(s2[:, 1, :], sp[:, 1, :], ACT.Square, scale=LOAD_FACTOR)
-        nc.scalar.activation(s4[:, 1, :], s2[:, 1, :], ACT.Square)
+        nc.scalar.activation(lg[:, 1, :], e1[:, 1, :], ACT.Ln)
 
-        neg_top = keep.tile([P, 2, TRIPS], F32)
-        sums = [psum.tile([P, 2, TRIPS], F32, name=f"sums{b}") for b in range(2)]
-        res = [keep.tile([P, TRIPS], F32, name=f"res{b}") for b in range(2)]
+        neg_top = keep.tile([P, U // D * 2], F32)
+        total = psum.tile([P, 2 * TRIPS], F32, name="bank4")
+        weighted = {}
         state = {}
 
         def gather_first(i):
@@ -145,79 +151,91 @@ def tile_picked_ybpr_time_p_kernel(
             nc.vector.tensor_copy(first[:], u[b][:].indirect(lka_t[:, 32 * h : 32 * (h + 1)]))
             state[i, "first"] = first
 
-        def gather_second(i):
+        def gather_second(i, name):
             b, h = divmod(i, 2)
-            ut = ring.tile([P, PIECE], F32, name="ut")
+            ut = keep.tile([P, PIECE], F32, name=name)
             nc.vector.tensor_tensor(
                 ut[:], u[b][:].indirect(lkb_t[:, 32 * h : 32 * (h + 1)]), state[i, "first"][:], ALU.add
             )
             state[i, "ut"] = ut
 
-        def shift(i):
-            b, h = divmod(i, 2)
+        def shift(i, banks):
             ut = state[i, "ut"]
-            top = neg_top[:, b, P * h : P * (h + 1)]
+            trips = slice(P * i, P * (i + 1))
+            top = neg_top[:, trips]
+            per = D // len(banks)
+            parts = [psum.tile([P, per, P], F32, name=name) for name in banks]
             nc.vector.tensor_reduce(
                 top, ut[:].rearrange("p (v d) -> p v d", d=D), AX.X, ALU.max, negate=True
             )
-            delta = psum.tile([P, D, P], F32, name=f"delta{i % 2}")
-            for d in range(D):
-                nc.tensor.matmul(delta[:, d, :], ut[:, d::D], ident[:], start=True, stop=False, is_transpose=True)
-                nc.tensor.matmul(delta[:, d, :], top, ident[:], start=False, stop=True, is_transpose=True)
-            ex = ring.tile([P, D, P], F32, name="ex")
-            nc.scalar.activation(ex[:], delta[:], ACT.Exp)
+            for k in range(per):
+                for j, part in enumerate(parts):
+                    nc.tensor.matmul(
+                        part[:, k, :], ut[:, j * per + k :: D], ident[:], start=True, stop=False, is_transpose=True
+                    )
+                for part in parts:
+                    nc.tensor.matmul(part[:, k, :], top, ident[:], start=False, stop=True, is_transpose=True)
+            ex = keep.tile([P, D, P], F32, name=f"ex{i}")
+            for j, part in enumerate(parts):
+                nc.scalar.activation(ex[:, j * per : (j + 1) * per, :], part[:], ACT.Exp)
             for d in range(D):
                 nc.tensor.matmul(
-                    sums[b][:, 0, P * h : P * (h + 1)], ex[:, d, :], ident[:],
-                    start=(d == 0), stop=(d == D - 1), is_transpose=True,
+                    total[:, trips], ex[:, d, :], ident[:], start=(d == 0), stop=(d == D - 1), is_transpose=True
                 )
-            state[i, "delta"] = delta
+            state[i, "parts"] = parts
             state[i, "ex"] = ex
 
-        def weigh(i):
+        def weigh(i, bank):
             b, h = divmod(i, 2)
-            pr = ring.tile([P, D, P], F32, name="pr")
-            nc.vector.tensor_tensor(pr[:], state[i, "delta"][:], state[i, "ex"][:], ALU.mult)
+            parts = state[i, "parts"]
+            per = D // len(parts)
+            pr = keep.tile([P, D, P], F32, name=f"pr{i}")
+            for j, part in enumerate(parts):
+                ds = slice(j * per, (j + 1) * per)
+                nc.vector.tensor_tensor(pr[:, ds, :], part[:], state[i, "ex"][:, ds, :], ALU.mult)
+            if bank is not None:
+                weighted[b] = psum.tile([P, TRIPS], F32, name=bank)
             for d in range(D):
                 nc.tensor.matmul(
-                    sums[b][:, 1, P * h : P * (h + 1)], pr[:, d, :], ident[:],
+                    weighted[b][:, P * h : P * (h + 1)], pr[:, d, :], ident[:],
                     start=(d == 0), stop=(d == D - 1), is_transpose=True,
                 )
 
-        def finish(b, c, inv_total):
-            mean = ring.tile([P, TRIPS], F32, name="mean")
-            nc.vector.scalar_tensor_tensor(
-                mean[:, c], sums[b][:, 1, c], inv_theta[:, b : b + 1], inv_total, ALU.mult, ALU.mult
-            )
-            nc.vector.scalar_tensor_tensor(
-                res[b][:, c], neg_top[:, b, c], neg_inv_theta[:, b : b + 1], mean[:, c], ALU.mult, ALU.add
-            )
-            nc.sync.dma_start(out=out[P * b : P * (b + 1), c], in_=res[b][:, c])
-
         gather_first(0)
-        nc.vector.scalar_tensor_tensor(u[1][:, :S], s4[:, 1, :], 1.0, g[:, 1, :], ALU.add, ALU.mult)
-        gather_second(0)
+        for h in range(2):
+            nc.vector.tensor_tensor(sp[:, cols[h]], y[1, h][:], lg[:, 1, cols[h]], ALU.max)
+        nc.scalar.activation(s2[:, 1, :], sp[:], ACT.Square, scale=LOAD_FACTOR)
+        nc.scalar.activation(s4[:, 1, :], s2[:, 1, :], ACT.Square)
+        slow = keep.tile([P, S], F32)
+        nc.scalar.activation(slow[:], s4[:, 1, :], ACT.Identity, bias=theta_nz[:, 1:2], scale=theta_nz[:, 1:2])
+        gather_second(0, "ut0")
         gather_first(1)
-        shift(0)
-        gather_second(1)
+        shift(0, ["bank5"])
+        gather_second(1, "ut1")
+        nc.vector.tensor_tensor(u[1][:, :S], slow[:], free_t[:], ALU.mult)
+        shift(1, ["bank6"])
         gather_first(2)
-        shift(1)
-        weigh(0)
-        gather_second(2)
+        gather_second(2, "ut2")
         gather_first(3)
-        weigh(1)
-        root = keep.tile([P, TRIPS], F32)
-        nc.scalar.activation(root[:], sums[0][:, 0, :], ACT.Abs_reciprocal_sqrt)
-        inv0 = keep.tile([P, TRIPS], F32)
-        nc.scalar.activation(inv0[:], root[:], ACT.Square)
-        shift(2)
-        gather_second(3)
-        finish(0, slice(0, TRIPS), inv0[:])
-        shift(3)
-        weigh(2)
-        inv1 = keep.tile([P, TRIPS], F32)
-        nc.vector.reciprocal(inv1[:, :P], sums[1][:, 0, :P])
-        finish(1, slice(0, P), inv1[:, :P])
-        weigh(3)
-        nc.vector.reciprocal(inv1[:, P:], sums[1][:, 0, P:])
-        finish(1, slice(P, TRIPS), inv1[:, P:])
+        shift(2, ["bank7"])
+        gather_second(3, "ut3")
+        shift(3, ["bank0", "bank1", "bank2", "bank3"])
+        weigh(0, "bank5")
+        weigh(1, None)
+        weigh(2, "bank7")
+        weigh(3, None)
+        top_total = keep.tile([P, 2 * TRIPS], F32)
+        nc.vector.tensor_tensor(top_total[:], total[:], neg_top[:], ALU.mult)
+        for b in range(2):
+            trips = slice(TRIPS * b, TRIPS * (b + 1))
+            numer = keep.tile([P, TRIPS], F32, name=f"numer{b}")
+            nc.vector.tensor_tensor(numer[:], weighted[b][:], top_total[:, trips], ALU.subtract)
+            root = keep.tile([P, TRIPS], F32, name=f"root{b}")
+            nc.scalar.activation(root[:], total[:, trips], ACT.Abs_reciprocal_sqrt)
+            inv_total = keep.tile([P, TRIPS], F32, name=f"inv_total{b}")
+            nc.scalar.activation(inv_total[:], root[:], ACT.Square)
+            res = keep.tile([P, TRIPS], F32, name=f"res{b}")
+            nc.vector.scalar_tensor_tensor(
+                res[:], numer[:], inv_theta[:, b : b + 1], inv_total[:], ALU.mult, ALU.mult
+            )
+            nc.sync.dma_start(out=out[P * b : P * (b + 1), :], in_=res[:])

@@ -47,19 +47,19 @@ def tile_picked_ybpr_time_p_kernel(
         w_raw = keep.tile([P, 4, N], F32)
         theta_t = keep.tile([P, 2], F32)
         free_t = keep.tile([P, S], F32)
+        free_col = keep.tile([P, S // P], F32)
 
-        nc.gpsimd.memset(scales[:].bitcast(I32), 0)
-        nc.sync.dma_start(offs_t[:], offs)
+        nc.vector.memset(scales[:].bitcast(I32), 0)
         nc.sync.dma_start(out=w_raw[:], in_=w1.rearrange("(p j) n -> p j n", j=4))
+        nc.sync.dma_start(offs_t[:], offs)
+        for r in range(4):
+            nc.sync.dma_start(out=scales[r:P:32, :].bitcast(I32), in_=x_scales[0, r:16:4, :].bitcast(I32))
+        nc.sync.dma_start(out=words[:], in_=x_words[0].rearrange("p n t -> p (n t)").bitcast(I32))
         with nc.allow_non_contiguous_dma(reason="one value a partition"):
             nc.sync.dma_start(out=theta_t[:], in_=theta.rearrange("(b p) o -> p (b o)", p=P))
-        for q in range(4):
-            nc.sync.dma_start(
-                out=scales[32 * q : 32 * q + 4, :].bitcast(I32),
-                in_=x_scales[0, 4 * q : 4 * q + 4, :].bitcast(I32),
-            )
-        nc.sync.dma_start(out=words[:], in_=x_words[0].rearrange("p n t -> p (n t)").bitcast(I32))
         nc.sync.dma_start(out=free_t[:], in_=free)
+        with nc.allow_non_contiguous_dma(reason="one value a partition"):
+            nc.sync.dma_start(out=free_col[:], in_=free[0:1, :].rearrange("o (t p) -> p (o t)", p=P))
         nc.sync.dma_start(lka_t[:], lka)
         nc.sync.dma_start(lkb_t[:], lkb)
 
@@ -71,7 +71,9 @@ def tile_picked_ybpr_time_p_kernel(
             nc.vector.memset(u[b][:, S:], 0.0)
 
         w_bf = keep.tile([P, N, 4], BF16, align_bytes=64)
-        nc.vector.tensor_copy(out=w_bf[:], in_=w_raw[:].rearrange("p j n -> p n j"))
+        nc.vector.tensor_copy(
+            out=w_bf[:].rearrange("p (c i) j -> p c j i", i=4), in_=w_raw[:].rearrange("p j (c i) -> p c j i", i=4)
+        )
         x_sc = keep.tile([P, S], U8, align_bytes=64)
         nc.vector.tensor_copy(x_sc[:], scales[:].indirect(offs_t[:]))
         w_q = keep.tile([P, N], U32, align_bytes=64)
@@ -81,14 +83,12 @@ def tile_picked_ybpr_time_p_kernel(
         )
 
         is_zero = keep.tile([P, 2], F32)
-        nc.vector.tensor_scalar(is_zero[:], theta_t[:], 0.0, THETA_FOR_ZERO, ALU.is_equal, ALU.mult)
+        nc.gpsimd.tensor_scalar(is_zero[:], theta_t[:], 0.0, THETA_FOR_ZERO, ALU.is_equal, ALU.mult)
         theta_nz = keep.tile([P, 2], F32)
-        nc.vector.tensor_tensor(theta_nz[:], theta_t[:], is_zero[:], ALU.add)
-        inv_theta = keep.tile([P, 2], F32)
-        nc.vector.reciprocal(inv_theta[:], theta_nz[:])
+        nc.gpsimd.tensor_tensor(theta_nz[:], theta_t[:], is_zero[:], ALU.add)
 
         theta_cap = keep.tile([P, 1], F32)
-        nc.vector.tensor_scalar(theta_cap[:], theta_nz[:, 0:1], 1.0 / CAP_TIME, 1.0, ALU.mult, ALU.mult)
+        nc.gpsimd.tensor_scalar(theta_cap[:], theta_nz[:, 0:1], 1.0 / CAP_TIME, 1.0, ALU.mult, ALU.mult)
 
         cols = [slice(HALF * h, HALF * (h + 1)) for h in range(2)]
         x_q = [keep.tile([P, HALF], U32, name=f"x_q{h}", align_bytes=64) for h in range(2)]
@@ -112,23 +112,28 @@ def tile_picked_ybpr_time_p_kernel(
                 nc.scalar.activation(e[:, b, cols[h]], y[b, h][:], ACT.Exp)
 
         big = keep.tile([P, S], F32)
-        for h in range(2):
-            nc.vector.tensor_scalar(big[:, cols[h]], y[0, h][:], LOG_CAP, LOAD_FACTOR, ALU.max, ALU.mult)
         big2 = keep.tile([P, S], F32)
-        nc.vector.tensor_tensor(big2[:], big[:], big[:], ALU.mult)
-        e1 = keep.tile([P, 2, S], F32)
-        nc.vector.tensor_scalar(e1[:], e[:], EXP_CAP, 1.0, ALU.min, ALU.add)
         big4 = keep.tile([P, S], F32)
-        nc.vector.tensor_tensor(big4[:], big2[:], big2[:], ALU.mult)
         over = keep.tile([P, S], F32)
-        nc.vector.tensor_scalar(over[:], big4[:], theta_cap[:], theta_cap[:], ALU.mult, ALU.add)
         g0 = keep.tile([P, S], F32)
-        nc.vector.tensor_tensor(g0[:], over[:], free_t[:], ALU.mult)
+        e1 = keep.tile([P, 2, S], F32)
+        for c, h in zip(cols, range(2)):
+            nc.vector.tensor_scalar(big[:, c], y[0, h][:], LOG_CAP, LOAD_FACTOR, ALU.max, ALU.mult)
+        for c in cols:
+            nc.vector.tensor_tensor(big2[:, c], big[:, c], big[:, c], ALU.mult)
+        nc.vector.tensor_scalar(e1[:], e[:], EXP_CAP, 1.0, ALU.min, ALU.add)
+        for c in cols:
+            nc.vector.tensor_tensor(big4[:, c], big2[:, c], big2[:, c], ALU.mult)
+        for c in cols:
+            nc.vector.tensor_scalar(over[:, c], big4[:, c], theta_cap[:], theta_cap[:], ALU.mult, ALU.add)
+        for c in cols:
+            nc.vector.tensor_tensor(g0[:, c], over[:, c], free_t[:, c], ALU.mult)
+        inv_theta = e[:, 0, 0:2]
+        nc.vector.reciprocal(inv_theta, theta_nz[:])
 
-        lg = keep.tile([P, 2, S], F32)
-        sp = keep.tile([P, S], F32)
-        s2 = keep.tile([P, 2, S], F32)
-        s4 = keep.tile([P, 2, S], F32)
+        lg = keep.tile([P, 1, S], F32)
+        s2 = keep.tile([P, 1, S], F32)
+        s4 = keep.tile([P, 1, S], F32)
         for h in range(2):
             nc.scalar.activation(lg[:, 0, cols[h]], e1[:, 0, cols[h]], ACT.Ln)
         for h in range(2):
@@ -138,104 +143,132 @@ def tile_picked_ybpr_time_p_kernel(
             nc.vector.scalar_tensor_tensor(
                 u[0][:, cols[h]], s4[:, 0, cols[h]], 1.0, g0[:, cols[h]], ALU.add, ALU.mult
             )
-        nc.scalar.activation(lg[:, 1, :], e1[:, 1, :], ACT.Ln)
+        lg1 = s2[:, 0, :]
+        excess = lg[:, 0, :]
+        for h in range(2):
+            nc.scalar.activation(excess[:, cols[h]], y[1, h][:], ACT.Relu, bias=-LOG_CAP)
+        for c in cols:
+            nc.scalar.activation(lg1[:, c], e1[:, 1, c], ACT.Ln)
 
-        neg_top = keep.tile([P, U // D * 2], F32)
-        total = psum.tile([P, 2 * TRIPS], F32, name="bank4")
+        ex = [keep.tile([P, PIECE], F32, name=f"ex{i}")[:] for i in range(4)]
+        ut = [keep.tile([P, PIECE], F32, name=f"ut{i}")[:] for i in range(3)]
+        neg_top = [keep.tile([P, TRIPS], F32, name=f"neg_top{b}")[:] for b in range(2)]
+        total = {}
         weighted = {}
-        state = {}
+        first = {}
+        delta = {}
+
+        def transpose_into(dst, src, start, stop):
+            nc.tensor.matmul(dst, src, ident[:], start=start, stop=stop, is_transpose=True)
 
         def gather_first(i):
             b, h = divmod(i, 2)
-            first = ring.tile([P, PIECE], F32, name="first")
-            nc.vector.tensor_copy(first[:], u[b][:].indirect(lka_t[:, 32 * h : 32 * (h + 1)]))
-            state[i, "first"] = first
+            first[i] = ring.tile([P, PIECE], F32, name="first")
+            nc.vector.tensor_copy(first[i][:], u[b][:].indirect(lka_t[:, 32 * h : 32 * (h + 1)]))
 
-        def gather_second(i, name):
+        def gather_second(i):
             b, h = divmod(i, 2)
-            ut = keep.tile([P, PIECE], F32, name=name)
             nc.vector.tensor_tensor(
-                ut[:], u[b][:].indirect(lkb_t[:, 32 * h : 32 * (h + 1)]), state[i, "first"][:], ALU.add
+                ut[i], u[b][:].indirect(lkb_t[:, 32 * h : 32 * (h + 1)]), first[i][:], ALU.add
             )
-            state[i, "ut"] = ut
 
-        def shift(i, banks):
-            ut = state[i, "ut"]
-            trips = slice(P * i, P * (i + 1))
-            top = neg_top[:, trips]
-            per = D // len(banks)
-            parts = [psum.tile([P, per, P], F32, name=name) for name in banks]
+        def shift(i, parts):
+            b, h = divmod(i, 2)
+            top = neg_top[b][:, P * h : P * (h + 1)]
+            per = D // len(parts)
             nc.vector.tensor_reduce(
-                top, ut[:].rearrange("p (v d) -> p v d", d=D), AX.X, ALU.max, negate=True
+                top, ut[i].rearrange("p (v d) -> p v d", d=D), AX.X, ALU.max, negate=True
             )
             for k in range(per):
                 for j, part in enumerate(parts):
-                    nc.tensor.matmul(
-                        part[:, k, :], ut[:, j * per + k :: D], ident[:], start=True, stop=False, is_transpose=True
-                    )
+                    transpose_into(part[:, P * k : P * (k + 1)], ut[i][:, j * per + k :: D], True, False)
                 for part in parts:
-                    nc.tensor.matmul(part[:, k, :], top, ident[:], start=False, stop=True, is_transpose=True)
-            ex = keep.tile([P, D, P], F32, name=f"ex{i}")
+                    transpose_into(part[:, P * k : P * (k + 1)], top, False, True)
             for j, part in enumerate(parts):
-                nc.scalar.activation(ex[:, j * per : (j + 1) * per, :], part[:], ACT.Exp)
-            for d in range(D):
-                nc.tensor.matmul(
-                    total[:, trips], ex[:, d, :], ident[:], start=(d == 0), stop=(d == D - 1), is_transpose=True
-                )
-            state[i, "parts"] = parts
-            state[i, "ex"] = ex
+                nc.scalar.activation(ex[i][:, P * per * j : P * per * (j + 1)], part, ACT.Exp)
+            delta[i] = parts
 
-        def weigh(i, bank):
-            b, h = divmod(i, 2)
-            parts = state[i, "parts"]
-            per = D // len(parts)
-            pr = keep.tile([P, D, P], F32, name=f"pr{i}")
-            for j, part in enumerate(parts):
-                ds = slice(j * per, (j + 1) * per)
-                nc.vector.tensor_tensor(pr[:, ds, :], part[:], state[i, "ex"][:, ds, :], ALU.mult)
-            if bank is not None:
-                weighted[b] = psum.tile([P, TRIPS], F32, name=bank)
+        def sum_routes(dst, src):
             for d in range(D):
-                nc.tensor.matmul(
-                    weighted[b][:, P * h : P * (h + 1)], pr[:, d, :], ident[:],
-                    start=(d == 0), stop=(d == D - 1), is_transpose=True,
-                )
+                transpose_into(dst, src[:, P * d : P * (d + 1)], d == 0, d == D - 1)
+
+        def add_up(i):
+            b, h = divmod(i, 2)
+            sum_routes(total[b][:, P * h : P * (h + 1)], ex[i])
+
+        def weigh(i):
+            width = PIECE // len(delta[i])
+            pr = keep.tile([P, PIECE], F32, name=f"pr{i}")
+            for j, part in enumerate(delta[i]):
+                c = slice(width * j, width * (j + 1))
+                nc.vector.tensor_tensor(pr[:, c], part, ex[i][:, c], ALU.mult)
+            return pr
+
+        def bank(number, width):
+            return psum.tile([P, width], F32, name=f"bank{number}")[:]
 
         gather_first(0)
-        for h in range(2):
-            nc.vector.tensor_tensor(sp[:, cols[h]], y[1, h][:], lg[:, 1, cols[h]], ALU.max)
-        nc.scalar.activation(s2[:, 1, :], sp[:], ACT.Square, scale=LOAD_FACTOR)
-        nc.scalar.activation(s4[:, 1, :], s2[:, 1, :], ACT.Square)
-        slow = keep.tile([P, S], F32)
-        nc.scalar.activation(slow[:], s4[:, 1, :], ACT.Identity, bias=theta_nz[:, 1:2], scale=theta_nz[:, 1:2])
-        gather_second(0, "ut0")
         gather_first(1)
-        shift(0, ["bank5"])
-        gather_second(1, "ut1")
-        nc.vector.tensor_tensor(u[1][:, :S], slow[:], free_t[:], ALU.mult)
-        shift(1, ["bank6"])
+        turned = [bank(4, HALF), bank(7, HALF)]
+        for h in range(2):
+            for t in range(2):
+                links = slice(HALF * h + P * t, HALF * h + P * (t + 1))
+                transpose_into(turned[h][:, P * t : P * (t + 1)], excess[:, links], True, False)
+                transpose_into(turned[h][:, P * t : P * (t + 1)], lg1[:, links], False, True)
+        square = keep.tile([P, S], F32)
+        fourth = keep.tile([P, S], F32)
+        for h in range(2):
+            nc.scalar.activation(square[:, cols[h]], turned[h], ACT.Square, scale=LOAD_FACTOR)
+        for c in cols:
+            nc.scalar.activation(fourth[:, c], square[:, c], ACT.Square)
+        for h in range(2):
+            back = bank(5 + h, HALF)
+            for t in range(2):
+                links = slice(HALF * h + P * t, HALF * h + P * (t + 1))
+                col = free_col[:, 2 * h + t : 2 * h + t + 1]
+                nc.scalar.activation(ex[0][:, links], fourth[:, links], ACT.Identity, bias=col, scale=col)
+                transpose_into(back[:, P * t : P * (t + 1)], ex[0][:, links], True, True)
+            nc.scalar.activation(u[1][:, cols[h]], back, ACT.Copy, scale=theta_nz[:, 1:2])
+        gather_second(0)
+        gather_second(1)
+        last_bank = bank(3, TRIPS + P)
+        total[0] = last_bank[:, :TRIPS]
+        shift(0, [bank(5, PIECE)])
+        add_up(0)
+        shift(1, [bank(6, PIECE)])
+        add_up(1)
         gather_first(2)
-        gather_second(2, "ut2")
         gather_first(3)
-        shift(2, ["bank7"])
-        gather_second(3, "ut3")
-        shift(3, ["bank0", "bank1", "bank2", "bank3"])
-        weigh(0, "bank5")
-        weigh(1, None)
-        weigh(2, "bank7")
-        weigh(3, None)
-        top_total = keep.tile([P, 2 * TRIPS], F32)
-        nc.vector.tensor_tensor(top_total[:], total[:], neg_top[:], ALU.mult)
+        gather_second(2)
+        shift(2, [bank(7, 2 * P), bank(4, 2 * P)])
+        ut.append(first[2][:])
+        gather_second(3)
+        shift(3, [bank(0, P), bank(1, P), bank(2, P), last_bank[:, TRIPS:]])
+        pr = weigh(0)
+        both = bank(5, 2 * TRIPS)
+        total[1] = both[:, :TRIPS]
+        weighted[0] = both[:, TRIPS:]
+        sum_routes(weighted[0][:, :P], pr)
+        sum_routes(weighted[0][:, P:], weigh(1))
+        add_up(2)
+        weighted[1] = bank(6, TRIPS)
+        pr2 = weigh(2)
+        add_up(3)
+        sum_routes(weighted[1][:, :P], pr2)
+        sum_routes(weighted[1][:, P:], weigh(3))
+        top_total = keep.tile([P, 2, TRIPS], F32)
+        numer = keep.tile([P, 2, TRIPS], F32)
+        root = keep.tile([P, 2, TRIPS], F32)
         for b in range(2):
-            trips = slice(TRIPS * b, TRIPS * (b + 1))
-            numer = keep.tile([P, TRIPS], F32, name=f"numer{b}")
-            nc.vector.tensor_tensor(numer[:], weighted[b][:], top_total[:, trips], ALU.subtract)
-            root = keep.tile([P, TRIPS], F32, name=f"root{b}")
-            nc.scalar.activation(root[:], total[:, trips], ACT.Abs_reciprocal_sqrt)
+            nc.vector.tensor_tensor(top_total[:, b, :], total[b], neg_top[b], ALU.mult)
+        for b in range(2):
+            nc.vector.tensor_tensor(numer[:, b, :], weighted[b], top_total[:, b, :], ALU.subtract)
+            nc.scalar.activation(root[:, b, :], total[b], ACT.Abs_reciprocal_sqrt)
+        for b in range(2):
             inv_total = keep.tile([P, TRIPS], F32, name=f"inv_total{b}")
-            nc.scalar.activation(inv_total[:], root[:], ACT.Square)
+            nc.scalar.activation(inv_total[:], root[:, b, :], ACT.Square)
             res = keep.tile([P, TRIPS], F32, name=f"res{b}")
             nc.vector.scalar_tensor_tensor(
-                res[:], numer[:], inv_theta[:, b : b + 1], inv_total[:], ALU.mult, ALU.mult
+                res[:], numer[:, b, :], inv_theta[:, b : b + 1], inv_total[:], ALU.mult, ALU.mult
             )
             nc.sync.dma_start(out=out[P * b : P * (b + 1), :], in_=res[:])

import math
from contextlib import ExitStack

import concourse.mybir as mybir
from concourse.masks import make_identity

F32 = mybir.dt.float32
BF16 = mybir.dt.bfloat16
I32 = mybir.dt.int32
U32 = mybir.dt.uint32
U16 = mybir.dt.uint16
U8 = mybir.dt.uint8
FP8X4 = mybir.dt.float8_e4m3fn_x4
ALU = mybir.AluOpType
ACT = mybir.ActivationFunctionType
AX = mybir.AxisListType

P = 128
K, T, S, N, U, D = 512, 2048, 512, 256, 1024, 4
HALF = S // 2
TRIPS = U // D
PIECE = P * D
SPARE = 8
EXP_CAP = 2.0 ** 60
LOAD_FACTOR = 0.9 * 0.15 ** 0.25
LOG_CAP = math.log(1.0 + EXP_CAP)
CAP_TIME = 1.0 + (LOAD_FACTOR * LOG_CAP) ** 4
THETA_FOR_ZERO = 2.0 ** -40

FLOPS = 2 * K * S * N


def tile_picked_ybpr_time_p_kernel(
    tc, x_words, x_scales, w1, free, theta, offs, lka, lkb, out
):
    nc = tc.nc
    with ExitStack() as ctx:
        keep = ctx.enter_context(tc.tile_pool(name="keep", bufs=1))
        ring = ctx.enter_context(tc.tile_pool(name="ring", bufs=2))
        psum = ctx.enter_context(tc.psum_pool(name="psum", bufs=1))

        offs_t = keep.tile([P, S // 16], U16)
        lka_t = keep.tile([P, U // 16], U16)
        lkb_t = keep.tile([P, U // 16], U16)
        words = keep.tile([P, T], I32, align_bytes=64)
        scales = keep.tile([P, T], U8, align_bytes=64)
        w_raw = keep.tile([P, 4, N], F32)
        theta_t = keep.tile([P, 2], F32)
        free_t = keep.tile([P, S], F32)
        free_col = keep.tile([P, S // P], F32)

        nc.vector.memset(scales[:].bitcast(I32), 0)
        nc.sync.dma_start(out=w_raw[:], in_=w1.rearrange("(p j) n -> p j n", j=4))
        nc.sync.dma_start(offs_t[:], offs)
        for r in range(4):
            nc.sync.dma_start(out=scales[r:P:32, :].bitcast(I32), in_=x_scales[0, r:16:4, :].bitcast(I32))
        nc.sync.dma_start(out=words[:], in_=x_words[0].rearrange("p n t -> p (n t)").bitcast(I32))
        with nc.allow_non_contiguous_dma(reason="one value a partition"):
            nc.sync.dma_start(out=theta_t[:], in_=theta.rearrange("(b p) o -> p (b o)", p=P))
        nc.sync.dma_start(out=free_t[:], in_=free)
        with nc.allow_non_contiguous_dma(reason="one value a partition"):
            nc.sync.dma_start(out=free_col[:], in_=free[0:1, :].rearrange("o (t p) -> p (o t)", p=P))
        nc.sync.dma_start(lka_t[:], lka)
        nc.sync.dma_start(lkb_t[:], lkb)

        ident = keep.tile([P, P], F32)
        make_identity(nc, ident[:])

        u = [keep.tile([P, S + SPARE], F32, name=f"u{b}") for b in range(2)]
        for b in range(2):
            nc.vector.memset(u[b][:, S:], 0.0)

        w_bf = keep.tile([P, N, 4], BF16, align_bytes=64)
        nc.vector.tensor_copy(
            out=w_bf[:].rearrange("p (c i) j -> p c j i", i=4), in_=w_raw[:].rearrange("p j (c i) -> p c j i", i=4)
        )
        x_sc = keep.tile([P, S], U8, align_bytes=64)
        nc.vector.tensor_copy(x_sc[:], scales[:].indirect(offs_t[:]))
        w_q = keep.tile([P, N], U32, align_bytes=64)
        w_sc = keep.tile([P, N], U8, align_bytes=64)
        nc.vector.quantize_mx(
            out=w_q[:].bitcast(FP8X4), scales=w_sc[:], in_=w_bf[:].rearrange("p n j -> p (n j)")
        )

        is_zero = keep.tile([P, 2], F32)
        nc.gpsimd.tensor_scalar(is_zero[:], theta_t[:], 0.0, THETA_FOR_ZERO, ALU.is_equal, ALU.mult)
        theta_nz = keep.tile([P, 2], F32)
        nc.gpsimd.tensor_tensor(theta_nz[:], theta_t[:], is_zero[:], ALU.add)

        theta_cap = keep.tile([P, 1], F32)
        nc.gpsimd.tensor_scalar(theta_cap[:], theta_nz[:, 0:1], 1.0 / CAP_TIME, 1.0, ALU.mult, ALU.mult)

        cols = [slice(HALF * h, HALF * (h + 1)) for h in range(2)]
        x_q = [keep.tile([P, HALF], U32, name=f"x_q{h}", align_bytes=64) for h in range(2)]
        y = {}
        e = keep.tile([P, 2, S], F32)
        for h in range(2):
            nc.vector.tensor_copy(
                x_q[h][:], words[:].bitcast(U32).indirect(offs_t[:, 16 * h : 16 * (h + 1)])
            )
            for b in range(2):
                y[b, h] = psum.tile([P, HALF], F32, name=f"bank{2 * b + h}")
                nc.tensor.matmul_mx(
                    out=y[b, h][:],
                    lhsT=w_q[:, P * b : P * (b + 1)].bitcast(FP8X4),
                    lhsT_scale=w_sc[:, P * b : P * (b + 1)],
                    rhs=x_q[h][:].bitcast(FP8X4),
                    rhs_scale=x_sc[:, cols[h]],
                    start=True,
                    stop=True,
                )
                nc.scalar.activation(e[:, b, cols[h]], y[b, h][:], ACT.Exp)

        big = keep.tile([P, S], F32)
        big2 = keep.tile([P, S], F32)
        big4 = keep.tile([P, S], F32)
        over = keep.tile([P, S], F32)
        g0 = keep.tile([P, S], F32)
        e1 = keep.tile([P, 2, S], F32)
        for c, h in zip(cols, range(2)):
            nc.vector.tensor_scalar(big[:, c], y[0, h][:], LOG_CAP, LOAD_FACTOR, ALU.max, ALU.mult)
        for c in cols:
            nc.vector.tensor_tensor(big2[:, c], big[:, c], big[:, c], ALU.mult)
        nc.vector.tensor_scalar(e1[:], e[:], EXP_CAP, 1.0, ALU.min, ALU.add)
        for c in cols:
            nc.vector.tensor_tensor(big4[:, c], big2[:, c], big2[:, c], ALU.mult)
        for c in cols:
            nc.vector.tensor_scalar(over[:, c], big4[:, c], theta_cap[:], theta_cap[:], ALU.mult, ALU.add)
        for c in cols:
            nc.vector.tensor_tensor(g0[:, c], over[:, c], free_t[:, c], ALU.mult)
        inv_theta = e[:, 0, 0:2]
        nc.vector.reciprocal(inv_theta, theta_nz[:])

        lg = keep.tile([P, 1, S], F32)
        s2 = keep.tile([P, 1, S], F32)
        s4 = keep.tile([P, 1, S], F32)
        for h in range(2):
            nc.scalar.activation(lg[:, 0, cols[h]], e1[:, 0, cols[h]], ACT.Ln)
        for h in range(2):
            nc.scalar.activation(s2[:, 0, cols[h]], lg[:, 0, cols[h]], ACT.Square, scale=LOAD_FACTOR)
        for h in range(2):
            nc.scalar.activation(s4[:, 0, cols[h]], s2[:, 0, cols[h]], ACT.Square)
            nc.vector.scalar_tensor_tensor(
                u[0][:, cols[h]], s4[:, 0, cols[h]], 1.0, g0[:, cols[h]], ALU.add, ALU.mult
            )
        lg1 = s2[:, 0, :]
        excess = lg[:, 0, :]
        for h in range(2):
            nc.scalar.activation(excess[:, cols[h]], y[1, h][:], ACT.Relu, bias=-LOG_CAP)
        for c in cols:
            nc.scalar.activation(lg1[:, c], e1[:, 1, c], ACT.Ln)

        ex = [keep.tile([P, PIECE], F32, name=f"ex{i}")[:] for i in range(4)]
        ut = [keep.tile([P, PIECE], F32, name=f"ut{i}")[:] for i in range(3)]
        neg_top = [keep.tile([P, TRIPS], F32, name=f"neg_top{b}")[:] for b in range(2)]
        total = {}
        weighted = {}
        first = {}
        delta = {}

        def transpose_into(dst, src, start, stop):
            nc.tensor.matmul(dst, src, ident[:], start=start, stop=stop, is_transpose=True)

        def gather_first(i):
            b, h = divmod(i, 2)
            first[i] = ring.tile([P, PIECE], F32, name="first")
            nc.vector.tensor_copy(first[i][:], u[b][:].indirect(lka_t[:, 32 * h : 32 * (h + 1)]))

        def gather_second(i):
            b, h = divmod(i, 2)
            nc.vector.tensor_tensor(
                ut[i], u[b][:].indirect(lkb_t[:, 32 * h : 32 * (h + 1)]), first[i][:], ALU.add
            )

        def shift(i, parts):
            b, h = divmod(i, 2)
            top = neg_top[b][:, P * h : P * (h + 1)]
            per = D // len(parts)
            nc.vector.tensor_reduce(
                top, ut[i].rearrange("p (v d) -> p v d", d=D), AX.X, ALU.max, negate=True
            )
            for k in range(per):
                for j, part in enumerate(parts):
                    transpose_into(part[:, P * k : P * (k + 1)], ut[i][:, j * per + k :: D], True, False)
                for part in parts:
                    transpose_into(part[:, P * k : P * (k + 1)], top, False, True)
            for j, part in enumerate(parts):
                nc.scalar.activation(ex[i][:, P * per * j : P * per * (j + 1)], part, ACT.Exp)
            delta[i] = parts

        def sum_routes(dst, src):
            for d in range(D):
                transpose_into(dst, src[:, P * d : P * (d + 1)], d == 0, d == D - 1)

        def add_up(i):
            b, h = divmod(i, 2)
            sum_routes(total[b][:, P * h : P * (h + 1)], ex[i])

        def weigh(i):
            width = PIECE // len(delta[i])
            pr = keep.tile([P, PIECE], F32, name=f"pr{i}")
            for j, part in enumerate(delta[i]):
                c = slice(width * j, width * (j + 1))
                nc.vector.tensor_tensor(pr[:, c], part, ex[i][:, c], ALU.mult)
            return pr

        def bank(number, width):
            return psum.tile([P, width], F32, name=f"bank{number}")[:]

        gather_first(0)
        gather_first(1)
        turned = [bank(4, HALF), bank(7, HALF)]
        for h in range(2):
            for t in range(2):
                links = slice(HALF * h + P * t, HALF * h + P * (t + 1))
                transpose_into(turned[h][:, P * t : P * (t + 1)], excess[:, links], True, False)
                transpose_into(turned[h][:, P * t : P * (t + 1)], lg1[:, links], False, True)
        square = keep.tile([P, S], F32)
        fourth = keep.tile([P, S], F32)
        for h in range(2):
            nc.scalar.activation(square[:, cols[h]], turned[h], ACT.Square, scale=LOAD_FACTOR)
        for c in cols:
            nc.scalar.activation(fourth[:, c], square[:, c], ACT.Square)
        for h in range(2):
            back = bank(5 + h, HALF)
            for t in range(2):
                links = slice(HALF * h + P * t, HALF * h + P * (t + 1))
                col = free_col[:, 2 * h + t : 2 * h + t + 1]
                nc.scalar.activation(ex[0][:, links], fourth[:, links], ACT.Identity, bias=col, scale=col)
                transpose_into(back[:, P * t : P * (t + 1)], ex[0][:, links], True, True)
            nc.scalar.activation(u[1][:, cols[h]], back, ACT.Copy, scale=theta_nz[:, 1:2])
        gather_second(0)
        gather_second(1)
        last_bank = bank(3, TRIPS + P)
        total[0] = last_bank[:, :TRIPS]
        shift(0, [bank(5, PIECE)])
        add_up(0)
        shift(1, [bank(6, PIECE)])
        add_up(1)
        gather_first(2)
        gather_first(3)
        gather_second(2)
        shift(2, [bank(7, 2 * P), bank(4, 2 * P)])
        ut.append(first[2][:])
        gather_second(3)
        shift(3, [bank(0, P), bank(1, P), bank(2, P), last_bank[:, TRIPS:]])
        pr = weigh(0)
        both = bank(5, 2 * TRIPS)
        total[1] = both[:, :TRIPS]
        weighted[0] = both[:, TRIPS:]
        sum_routes(weighted[0][:, :P], pr)
        sum_routes(weighted[0][:, P:], weigh(1))
        add_up(2)
        weighted[1] = bank(6, TRIPS)
        pr2 = weigh(2)
        add_up(3)
        sum_routes(weighted[1][:, :P], pr2)
        sum_routes(weighted[1][:, P:], weigh(3))
        top_total = keep.tile([P, 2, TRIPS], F32)
        numer = keep.tile([P, 2, TRIPS], F32)
        root = keep.tile([P, 2, TRIPS], F32)
        for b in range(2):
            nc.vector.tensor_tensor(top_total[:, b, :], total[b], neg_top[b], ALU.mult)
        for b in range(2):
            nc.vector.tensor_tensor(numer[:, b, :], weighted[b], top_total[:, b, :], ALU.subtract)
            nc.scalar.activation(root[:, b, :], total[b], ACT.Abs_reciprocal_sqrt)
        for b in range(2):
            inv_total = keep.tile([P, TRIPS], F32, name=f"inv_total{b}")
            nc.scalar.activation(inv_total[:], root[:, b, :], ACT.Square)
            res = keep.tile([P, TRIPS], F32, name=f"res{b}")
            nc.vector.scalar_tensor_tensor(
                res[:], numer[:, b, :], inv_theta[:, b : b + 1], inv_total[:], ALU.mult, ALU.mult
            )
            nc.sync.dma_start(out=out[P * b : P * (b + 1), :], in_=res[:])
